import numpy as np
import ml_dtypes


def mxq(x, axis, fmt="e4m3"):
    dtype, down = {"e4m3": (ml_dtypes.float8_e4m3fn, 7), "e5m2": (ml_dtypes.float8_e5m2, 14)}[fmt]
    v = np.moveaxis(np.asarray(x, np.float32).astype(ml_dtypes.bfloat16).astype(np.float64), axis, -1)
    blocks = v.reshape(v.shape[:-1] + (-1, 32))
    amax = np.abs(blocks).max(-1, keepdims=True)
    byte = np.maximum(np.where(amax > 0, np.frexp(amax)[1] - 1 + 127, 0) - down, 1)
    scale = np.exp2(byte - 127.0)
    codes = (blocks / scale).astype(np.float32).astype(dtype).astype(np.float64)
    return np.moveaxis((codes * scale).reshape(v.shape), -1, axis)


WIDE = False


def mx_kscale(k):
    if not WIDE:
        return np.ones(k)
    levels = np.array([10, -10, 5, -5, 0])
    if k % 512:
        return np.exp2(np.random.permutation(np.resize(levels, k // 32))).repeat(32)
    a = np.empty((k // 512, 16))
    for p in range(k // 512):
        a[p, :8] = np.random.permutation(np.resize(levels, 8))
        for g in range(8):
            far = levels[np.abs(levels - a[p, g]) >= 10]
            a[p, g + 8] = far[np.random.randint(len(far))]
    return np.exp2(a.ravel()).repeat(32)


BF16 = ml_dtypes.bfloat16


def bf(x):
    return np.asarray(x, np.float32).astype(BF16)


def f64(x):
    return np.asarray(x).astype(np.float64)

E4M3FN = np.array([(-1.0 if i & 128 else 1.0) * ((1.0 + (i & 7) / 8.0) * 2.0 ** (((i >> 3) & 15) - 7) if i & 120 else (i & 7) * 2.0 ** -9) for i in range(256)])


def e4m3fn_bytes(y):
    return np.clip(np.asarray(y, np.float64), -448.0, 448.0).astype(np.float32).astype(ml_dtypes.float8_e4m3fn).view(np.uint8)


def e4m3fn_values(b):
    return E4M3FN[b]


T, K, N, P, B = 2048, 2048, 1024, 128, 128
TOP = 448.0


def setup_inputs():
    s = mx_kscale(K)
    mu = 0.7 * np.random.standard_normal((P, K))
    x = (np.repeat(mu, T // P, axis=0) + np.random.standard_normal((T, K))) * s
    w = np.random.standard_normal((K, N)) / np.sqrt(K) / s[:, None]
    x_scale = (np.abs(x).reshape(T, K // B, B).max(axis=2) / TOP).astype(np.float32)
    w_scale = (np.abs(w).reshape(K // B, B, N // B, B).max(axis=(1, 3)) / TOP).astype(np.float32)
    return {"x_bytes": e4m3fn_bytes(x / np.repeat(f64(x_scale), B, axis=1)),
            "x_scale": x_scale,
            "w_bytes": e4m3fn_bytes(w / np.repeat(np.repeat(f64(w_scale), B, axis=0), B, axis=1)),
            "w_scale": w_scale,
            "means": bf(mu * s),
            "gain": bf(1 + 0.1 * np.random.standard_normal(N))}


def reference(x_bytes, x_scale, w_bytes, w_scale, means, gain):
    x = e4m3fn_values(x_bytes) * np.repeat(f64(x_scale), B, axis=1)
    w = e4m3fn_values(w_bytes) * np.repeat(np.repeat(f64(w_scale), B, axis=0), B, axis=1)
    wq = mxq(w, 0, "e4m3")
    raw = mxq(x, 1, "e4m3") @ wq
    centre = mxq(f64(means), 1, "e4m3") @ wq
    scores = raw.reshape(P, T // P, N) - centre[:, None, :]
    return (scores * f64(gain)).reshape(T, N)

from contextlib import ExitStack

import concourse.mybir as mybir
from concourse.masks import make_identity

T, K, N, PLATES = 2048, 2048, 1024, 128
FLOPS = 2 * T * K * N + 2 * PLATES * K * N

F32 = mybir.dt.float32
BF16 = mybir.dt.bfloat16
U32 = mybir.dt.uint32
U8 = mybir.dt.uint8
F8 = mybir.dt.float8_e4m3fn
X4 = mybir.dt.float8_e4m3fn_x4
ALU = mybir.AluOpType
COPY = mybir.ActivationFunctionType.Copy

P = 128
R = T // PLATES
G = K // 512
C = K // 128
H = 2
NH = N // H

VB = [12, 10, 6, 4, 8, 8, 6, 5, 5, 3, 1, 2, 4, 4, 7, 2]
WV = [1, 0, 0, 0, 0, 1, 0, 0]
EX = ["S"] * 34
GA = ["V"] * 32
LAG = 4
AHEAD = 2
HEADX = 2


def tile_plate_centred_gene_scores_d2_kernel(tc, x_bytes, x_scale, w_bytes, w_scale, means, gain, out):
    nc = tc.nc
    with ExitStack() as ctx:
        keep = ctx.enter_context(tc.tile_pool(name="keep", bufs=1))
        work = ctx.enter_context(tc.tile_pool(name="work", bufs=3))
        outs = ctx.enter_context(tc.tile_pool(name="outs", bufs=6))
        turn = ctx.enter_context(tc.psum_pool(name="turn", bufs=4))
        accs = ctx.enter_context(tc.psum_pool(name="accs", bufs=4))

        ident = keep.tile([P, P], F32, name="ident")
        make_identity(nc, ident[:])

        x_rows = x_bytes.rearrange("(p r) k -> p r k", r=R)
        out_rows = out.rearrange("(p r) n -> p r n", r=R)

        xs = keep.tile([P, R, C], F32, name="xs")
        wsb = keep.tile([P, G * 4 * 8], F32, name="wsb")
        ws = keep.tile([P, G, 8], F32, name="ws")
        gain_b = keep.tile([P, N], BF16, name="gain_b")
        mw = keep.tile([P, K], BF16, name="mw")
        cen = keep.tile([P, N], F32, name="cen")

        w_raw = {}
        for h in range(H):
            for g in range(G):
                w_raw[h, g] = keep.tile([P, 4, NH], U8, name="wb%d%d" % (h, g))
        x_raw = [keep.tile([P, K], U8, name="xb%d" % r) for r in range(2)]
        x_raw2 = [keep.tile([P, 2, K], U8, name="xp%d" % i) for i in range(1, R // 2)]

        def load_w(h, g):
            nc.sync.dma_start(
                out=w_raw[h, g][:],
                in_=w_bytes[512 * g : 512 * g + 512, NH * h : NH * h + NH].rearrange("(p t) n -> p t n", t=4),
            )

        def xb(r):
            if r < 2:
                return x_raw[r][:]
            return x_raw2[r // 2 - 1][:, r % 2, :]

        nc.sync.dma_start(out=wsb[:], in_=w_scale.rearrange("c d -> (c d)").partition_broadcast(P))
        load_w(0, 0)
        nc.sync.dma_start(out=xs[:], in_=x_scale.rearrange("(p r) c -> p r c", r=R))
        nc.sync.dma_start(out=x_raw[0][:], in_=x_rows[:, 0, :])
        load_w(0, 1)
        nc.sync.dma_start(out=mw[:], in_=means)
        load_w(0, 2)
        load_w(0, 3)
        nc.sync.dma_start(out=x_raw[1][:], in_=x_rows[:, 1, :])
        nc.sync.dma_start(out=x_raw2[0][:], in_=x_rows[:, 2:4, :])
        load_w(1, 0)
        load_w(1, 1)
        nc.sync.dma_start(out=gain_b[:], in_=gain.partition_broadcast(P))
        nc.sync.dma_start(out=x_raw2[1][:], in_=x_rows[:, 4:6, :])
        load_w(1, 2)
        load_w(1, 3)
        for i in range(3, R // 2):
            nc.sync.dma_start(out=x_raw2[i - 1][:], in_=x_rows[:, 2 * i : 2 * i + 2, :])

        for q in range(4):
            nc.vector.tensor_copy(
                out=ws[32 * q : 32 * q + 32, :, :],
                in_=wsb[32 * q : 32 * q + 32, :].rearrange("p (g q d) -> p g q d", q=4, d=8)[:, :, q, :],
            )

        w_codes, w_scales, w_wide, w_grp = {}, {}, {}, {}

        def widen_w(h, g):
            t = work.tile([P, 4 * NH], BF16, name="ww")
            src = w_raw[h, g][:].rearrange("p t n -> p (t n)").bitcast(F8)
            if WV[4 * h + g]:
                nc.vector.tensor_copy(out=t[:], in_=src)
            else:
                nc.scalar.copy(out=t[:], in_=src)
            w_wide[h, g] = t

        def scale_w(h, g):
            t = work.tile([P, NH * 4], BF16, name="wg", align_bytes=64)
            src = w_wide[h, g][:].rearrange("p (t n) -> p n t", t=4)
            dst = t[:].rearrange("p (n t) -> p n t", t=4)
            for d in range(4):
                nc.vector.tensor_scalar(
                    out=dst[:, 128 * d : 128 * d + 128, :],
                    in0=src[:, 128 * d : 128 * d + 128, :],
                    scalar1=ws[:, g, 4 * h + d : 4 * h + d + 1],
                    scalar2=None,
                    op0=ALU.mult,
                )
            w_grp[h, g] = t

        def quant_w(h, g):
            codes = keep.tile([P, NH], U32, name="wc%d%d" % (h, g), align_bytes=64)
            scales = keep.tile([P, NH], U8, name="wq%d%d" % (h, g), align_bytes=64)
            nc.vector.quantize_mx(out=codes[:].bitcast(X4), scales=scales[:], in_=w_grp[h, g][:])
            w_codes[h, g] = codes
            w_scales[h, g] = scales

        wide, grp, banks, codes_x, scales_x = {}, {}, {}, {}, {}
        wide[R] = mw

        def widen_x(r, vblocks):
            t = work.tile([P, K], BF16, name="xw")
            src = xb(r)
            for c in range(C):
                cols = slice(128 * c, 128 * c + 128)
                if c < vblocks:
                    nc.vector.tensor_scalar(
                        out=t[:, cols], in0=src[:, cols].bitcast(F8), scalar1=xs[:, r, c : c + 1], scalar2=None, op0=ALU.mult
                    )
                else:
                    nc.scalar.activation(out=t[:, cols], in_=src[:, cols].bitcast(F8), func=COPY, scale=xs[:, r, c : c + 1])
            wide[r] = t

        def turn_x(r):
            words = wide[r][:].bitcast(F32)
            for b in range(2):
                pt = turn.tile([P, 2, 2, P], F32, name="pt")
                for j in range(2):
                    for u in range(2):
                        g = 2 * b + j
                        nc.tensor.transpose(pt[:, j, u, :], words[:, 256 * g + u : 256 * g + 256 : 2], ident[:])
                banks[r, b] = pt

        def exit_x(r, b, eng):
            if b == 0:
                grp[r] = work.tile([P, G * P * 4], BF16, name="xg", align_bytes=64)
            dst = grp[r][:, 1024 * b : 1024 * b + 1024].bitcast(F32).rearrange("p (j s u) -> p j s u", j=2, u=2)
            src = banks[r, b][:].rearrange("p j u s -> p j s u")
            if eng == "S":
                nc.scalar.copy(out=dst, in_=src)
            else:
                nc.vector.tensor_copy(out=dst, in_=src)

        def quant_x(r):
            codes = work.tile([P, G * P], U32, name="xc", align_bytes=64, bufs=8)
            scales = work.tile([P, G * P], U8, name="xq", align_bytes=64, bufs=8)
            nc.vector.quantize_mx(out=codes[:].bitcast(X4), scales=scales[:], in_=grp[r][:])
            codes_x[r] = codes
            scales_x[r] = scales

        acc = {}

        def mm(r, h):
            t = accs.tile([P, NH], F32, name="acc")
            for g in range(G):
                rows = slice(P * g, P * g + P)
                nc.tensor.matmul_mx(
                    out=t[:],
                    lhsT=codes_x[r][:, rows].bitcast(X4),
                    lhsT_scale=scales_x[r][:, rows],
                    rhs=w_codes[h, g][:].bitcast(X4),
                    rhs_scale=w_scales[h, g][:],
                    start=(g == 0),
                    stop=(g == G - 1),
                )
            acc[r, h] = t

        diffs = {}

        def sub(r, h):
            t = outs.tile([P, NH], F32, name="diff")
            cols = slice(NH * h, NH * h + NH)
            nc.vector.tensor_tensor(out=t[:], in0=acc[r, h][:], in1=cen[:, cols], op=ALU.subtract)
            diffs[r, h] = t

        def scale_out(r, h, eng):
            t = outs.tile([P, NH], F32, name="res")
            cols = slice(NH * h, NH * h + NH)
            e = nc.vector if eng == "V" else nc.gpsimd
            e.tensor_tensor(out=t[:], in0=diffs[r, h][:], in1=gain_b[:, cols], op=ALU.mult)
            nc.sync.dma_start(out=out_rows[:, r, cols], in_=t[:])

        def centre(h):
            mm(R, h)
            nc.scalar.copy(out=cen[:, NH * h : NH * h + NH], in_=acc[R, h][:])

        def prep(r, part):
            if part == 0:
                if r < R:
                    widen_x(r, VB[r])
                turn_x(r)
            elif part == 1:
                for b in range(2):
                    exit_x(r, b, EX[2 * r + b])
            else:
                quant_x(r)

        def head():
            widen_w(0, 0)
            prep(0, 0)
            scale_w(0, 0)
            widen_w(0, 1)
            prep(0, 1)
            scale_w(0, 1)
            quant_w(0, 0)
            widen_w(0, 2)
            prep(0, 2)
            scale_w(0, 2)
            quant_w(0, 1)
            widen_w(0, 3)
            prep(R, 0)
            prep(R, 1)
            scale_w(0, 3)
            quant_w(0, 2)
            prep(R, 2)
            quant_w(0, 3)
            for r in range(1, 1 + HEADX):
                for part in range(3):
                    prep(r, part)
            centre(0)

        def steady():
            for s in range(R + LAG):
                if s < R:
                    mm(s, 0)
                if s >= LAG:
                    mm(s - LAG, 1)
                n = s + HEADX + 1
                if n < R:
                    prep(n, 0)
                    prep(n, 1)
                if s < R:
                    sub(s, 0)
                if s >= LAG:
                    sub(s - LAG, 1)
                if n < R:
                    prep(n, 2)
                if s < G:
                    widen_w(1, s)
                    scale_w(1, s)
                    quant_w(1, s)
                if s == G - 1:
                    centre(1)
                if s < R:
                    scale_out(s, 0, GA[2 * s])
                if s >= LAG:
                    scale_out(s - LAG, 1, GA[2 * (s - LAG) + 1])

        head()
        steady()
